import numpy as np, ml_dtypes
CORES = [100,101,102,103,108,109,110,111]
N = 8
R, TK = 16, 512
def setup_inputs(rng):
    u = (rng.standard_normal((N, 128, R), dtype=np.float32) / 11).astype(ml_dtypes.bfloat16)
    return {"x": rng.standard_normal((N, 128, TK), dtype=np.float32).astype(ml_dtypes.bfloat16), "u": u, "ut": u.transpose(0, 2, 1).copy(), "vt": rng.standard_normal((N, R, 128), dtype=np.float32).astype(ml_dtypes.bfloat16)}
def setup_inputs_big(rng):
    d = setup_inputs(rng)
    for k in ("x", "u", "ut", "vt"): d[k] = (d[k].astype(np.float32) * 1024.0).astype(d[k].dtype)
    return d
def setup_inputs_small(rng):
    d = setup_inputs(rng)
    for k in ("x", "u", "ut", "vt"): d[k] = (d[k].astype(np.float32) * (1 / 1024.0)).astype(d[k].dtype)
    return d
def setup_inputs_apart(rng):
    d = setup_inputs(rng)
    f = (10.0 ** rng.permutation(np.linspace(-1.5, 1.5, N))).astype(np.float32).reshape(N, 1, 1)
    for k in ("x", "u", "ut", "vt"): d[k] = (d[k].astype(np.float32) * f).astype(d[k].dtype)
    return d
def tie_inputs(x):
    x = dict(x)
    x["ut"] = x["u"].transpose(0, 2, 1).copy()
    return x
def reference(x, u, ut, vt):
    X, U, VT = x.astype(np.float64), u.astype(np.float64), vt.astype(np.float64)
    y = np.stack([sum(VT[j].T @ (U[j].T @ X[r]) for j in range(N)) for r in range(N)])
    return {"y": y.astype(ml_dtypes.bfloat16 if x.dtype != np.float64 else np.float64)}

@@ -1,0 +1,144 @@
+import comms_topo
+from concourse.bass import DstId, RemoteDMATransfer
+
+CORES = [100, 101, 102, 103, 108, 109, 110, 111]
+P, R, TK = 128, 16, 512
+NCH = 2
+CW = TK // NCH
+SLOTS = max(sum(1 for d in CORES if comms_topo.chip(d) == comms_topo.chip(c)) for c in CORES) - 1
+
+SCRATCH = {
+    "utb": ("sbuf", [R, P], "bfloat16"),
+    "vtb": ("sbuf", [R, P], "bfloat16"),
+    "xb": ("sbuf", [P, TK], "bfloat16"),
+    "wown": ("sbuf", [P, P], "bfloat16"),
+    "wpeer": ("sbuf", [P, SLOTS * P], "bfloat16"),
+    "woff": ("sbuf", [P, P], "bfloat16"),
+    "yb": ("sbuf", [P, TK], "bfloat16"),
+    "pw": ("psum", [P, 512], "float32"),
+    "py0": ("psum", [P, 512], "float32"),
+    "py1": ("psum", [P, 512], "float32"),
+}
+SEMAPHORES = ["fac", "xl", "mmw", "cw", "on", "off", "sent", "my0", "my1", "cy0", "cy1", "st"]
+
+
+def _engs(topo, src, dst):
+    m = topo.mask(src, dst)
+    return [e for e in range(m.bit_length()) if (m >> e) & 1]
+
+
+def _bits(es):
+    return sum(1 << e for e in es)
+
+
+def _split(es, dsts):
+    if not dsts:
+        return []
+    n = 1
+    while 2 * n * len(dsts) <= len(es):
+        n *= 2
+    return [(d, es[i * n:(i + 1) * n]) for i, d in enumerate(dsts)]
+
+
+def _sides(topo, group, c):
+    near = [d for d in group if topo.chip(d) == topo.chip(c)]
+    far = [d for d in group if topo.chip(d) != topo.chip(c)]
+    ports = [d for d in near if all(topo.may_write(d, f) for f in far)]
+    return near, far, ports
+
+
+def _near_calls(topo, group, s):
+    near, far, ports = _sides(topo, group, s)
+    others = [c for c in near if c != s]
+    urgent = [c for c in others if c in ports]
+    later = [c for c in others if c not in ports]
+    every = _engs(topo, s, others[0])
+    if s in ports:
+        out = _engs(topo, s, far[0])
+        rest = [e for e in every if e not in out]
+        calls = [_split(out, urgent), _split(rest, later)]
+    else:
+        calls = [_split(every, urgent), _split(every, later)]
+    return [c for c in calls if c]
+
+
+def _far_share(topo, group, s):
+    near, far, ports = _sides(topo, group, s)
+    return far[ports.index(s)::len(ports)]
+
+
+def rank_program(g, core, T, topo):
+    if T.rank_of(core) is None:
+        return
+    S = T.sem
+    group = list(T.cores)
+    near, far, ports = _sides(topo, group, core)
+    others = [c for c in near if c != core]
+
+    def slot(dst, src):
+        k = [c for c in near if c != dst].index(src)
+        return T.wpeer[:, k * P:(k + 1) * P]
+
+    def did(c):
+        rid, pid, _ = topo.addr(c)
+        return DstId(rid=rid, pnc=pid)
+
+    on_total = sum(len(es) for s in others for call in _near_calls(topo, group, s) for d, es in call if d == core)
+    feeder = [s for s in _sides(topo, group, far[0])[2] if core in _far_share(topo, group, s)][0]
+    off_total = len(_engs(topo, feeder, core))
+
+    g.sync.dma_start(T.utb[:, :], T.ut[:, :]).then_inc(S.fac, 16)
+    g.scalar.dma_start(T.vtb[:, :], T.vt[:, :]).then_inc(S.fac, 16)
+    g.sync.dma_start(T.xb[:, 0:CW], T.x[:, 0:CW]).then_inc(S.xl, 16)
+    g.scalar.dma_start(T.xb[:, CW:TK], T.x[:, CW:TK]).then_inc(S.xl, 16)
+
+    g.tensor.wait_ge(S.fac, 32)
+    g.tensor.matmul(T.pw[:, 0:P], T.utb[:, :], T.vtb[:, :], True, True).then_inc(S.mmw, 1)
+    g.vector.wait_ge(S.mmw, 1)
+    g.vector.tensor_copy(T.wown[:, :], T.pw[:, 0:P]).then_inc(S.cw, 1)
+
+    sent = 0
+    g.wait_ge(S.cw, 1)
+    for call in _near_calls(topo, group, core):
+        g.remote_dma_fused(
+            [RemoteDMATransfer(dst_ids=[did(d)], dma_engine_mask=_bits(es), remote_sem=S.on,
+                               src=T.wown[:, :], dst=slot(d, core)) for d, es in call],
+            local_sem=S.sent)
+        sent += sum(len(es) for d, es in call)
+    g.wait_ge(S.on, on_total)
+    if core in ports:
+        share = _far_share(topo, group, core)
+        es = _engs(topo, core, share[0])
+        g.remote_dma_fused(
+            [RemoteDMATransfer(dst_ids=[did(d) for d in share], dma_engine_mask=_bits(es), remote_sem=S.off,
+                               srcs=[T.wown[:, :]] + [slot(core, s) for s in others],
+                               dsts=[T.woff[:, :] for d in share], alu_op=1)],
+            local_sem=S.sent)
+        sent += len(es)
+
+    py = [T.py0, T.py1]
+    my = [S.my0, S.my1]
+    cy = [S.cy0, S.cy1]
+    xs = [T.xb[:, b * CW:(b + 1) * CW] for b in range(NCH)]
+    g.tensor.wait_ge(S.cw, 1)
+    g.tensor.wait_ge(S.xl, 32)
+    for b in range(NCH):
+        g.tensor.matmul(py[b][:, 0:CW], T.wown[:, :], xs[b], True, False)
+    g.tensor.wait_ge(S.on, on_total)
+    for s in others:
+        for b in range(NCH):
+            g.tensor.matmul(py[b][:, 0:CW], slot(core, s), xs[b], False, False)
+    g.tensor.wait_ge(S.off, off_total)
+    for b in range(NCH):
+        g.tensor.matmul(py[b][:, 0:CW], T.woff[:, :], xs[b], False, True).then_inc(my[b], 1)
+
+    queues = [g.sync, g.scalar]
+    for b in range(NCH):
+        g.vector.wait_ge(my[b], 1)
+        g.vector.tensor_copy(T.yb[:, b * CW:(b + 1) * CW], py[b][:, 0:CW]).then_inc(cy[b], 1)
+        queues[b].wait_ge(cy[b], 1)
+        queues[b].dma_start(T.y[:, b * CW:(b + 1) * CW], T.yb[:, b * CW:(b + 1) * CW]).then_inc(S.st, 16)
+
+    g.wait_ge(S.sent, sent)
+    g.wait_ge(S.off, off_total)
+    g.wait_ge(S.st, 16 * NCH)

@@ -1,25 +1,34 @@
 import comms_topo
 from concourse.bass import DstId, RemoteDMATransfer
+from concourse.mybir import ActivationFunctionType
 
 CORES = [100, 101, 102, 103, 108, 109, 110, 111]
 P, R, TK = 128, 16, 512
-NCH = 2
-CW = TK // NCH
+PW = 2 * R
+HR = P // 2
+NB = 4
+CW = TK // NB
 SLOTS = max(sum(1 for d in CORES if comms_topo.chip(d) == comms_topo.chip(c)) for c in CORES) - 1
 
 SCRATCH = {
-    "utb": ("sbuf", [R, P], "bfloat16"),
-    "vtb": ("sbuf", [R, P], "bfloat16"),
+    "fac": ("dram", [SLOTS + 1, P, PW], "bfloat16"),
+    "fu": ("sbuf", [(SLOTS + 1) * R, P], "bfloat16"),
+    "fv": ("sbuf", [(SLOTS + 1) * R, P], "bfloat16"),
     "xb": ("sbuf", [P, TK], "bfloat16"),
     "wown": ("sbuf", [P, P], "bfloat16"),
+    "wnear": ("sbuf", [P, P], "bfloat16"),
     "wpeer": ("sbuf", [P, SLOTS * P], "bfloat16"),
     "woff": ("sbuf", [P, P], "bfloat16"),
     "yb": ("sbuf", [P, TK], "bfloat16"),
     "pw": ("psum", [P, 512], "float32"),
+    "pn": ("psum", [P, 512], "float32"),
     "py0": ("psum", [P, 512], "float32"),
     "py1": ("psum", [P, 512], "float32"),
+    "py2": ("psum", [P, 512], "float32"),
+    "py3": ("psum", [P, 512], "float32"),
 }
-SEMAPHORES = ["fac", "xl", "mmw", "cw", "on", "off", "sent", "my0", "my1", "cy0", "cy1", "st"]
+SEMAPHORES = ["stg", "ld", "xl", "mmw", "cw", "thin", "l2", "mmn", "cn", "on", "off", "sent",
+              "my0", "my1", "my2", "my3", "cy0", "cy1", "cy2", "cy3", "st"]
 
 
 def _engs(topo, src, dst):
@@ -47,23 +56,23 @@ def _sides(topo, group, c):
     return near, far, ports
 
 
-def _near_calls(topo, group, s):
+def _use(topo, group, s):
     near, far, ports = _sides(topo, group, s)
-    others = [c for c in near if c != s]
-    urgent = [c for c in others if c in ports]
-    later = [c for c in others if c not in ports]
-    every = _engs(topo, s, others[0])
-    if s in ports:
-        out = _engs(topo, s, far[0])
-        rest = [e for e in every if e not in out]
-        calls = [_split(out, urgent), _split(rest, later)]
-    else:
-        calls = [_split(every, urgent), _split(every, later)]
-    return [c for c in calls if c]
+    return _engs(topo, s, far[0]) if s in ports else _engs(topo, s, [c for c in near if c != s][0])
+
+
+def _thin_dsts(topo, group, s):
+    near, _, ports = _sides(topo, group, s)
+    return [c for c in near if c != s and c not in ports]
+
+
+def _w_writes(topo, group, s):
+    _, _, ports = _sides(topo, group, s)
+    return _split(_use(topo, group, s), [c for c in ports if c != s])
 
 
 def _far_share(topo, group, s):
-    near, far, ports = _sides(topo, group, s)
+    _, far, ports = _sides(topo, group, s)
     return far[ports.index(s)::len(ports)]
 
 
@@ -74,71 +83,111 @@ def rank_program(g, core, T, topo):
     group = list(T.cores)
     near, far, ports = _sides(topo, group, core)
     others = [c for c in near if c != core]
+    is_port = core in ports
+    use = _use(topo, group, core)
 
-    def slot(dst, src):
-        k = [c for c in near if c != dst].index(src)
+    def idx(dst, src):
+        return [c for c in near if c != dst].index(src)
+
+    def wslot(dst, src):
+        k = idx(dst, src)
         return T.wpeer[:, k * P:(k + 1) * P]
 
     def did(c):
         rid, pid, _ = topo.addr(c)
         return DstId(rid=rid, pnc=pid)
 
-    on_total = sum(len(es) for s in others for call in _near_calls(topo, group, s) for d, es in call if d == core)
+    thin_total = sum(len(_use(topo, group, s)) for s in others if core in _thin_dsts(topo, group, s))
+    on_total = sum(len(es) for s in others for d, es in _w_writes(topo, group, s) if d == core)
     feeder = [s for s in _sides(topo, group, far[0])[2] if core in _far_share(topo, group, s)][0]
-    off_total = len(_engs(topo, feeder, core))
+    off_total = len(_use(topo, group, feeder))
 
-    g.sync.dma_start(T.utb[:, :], T.ut[:, :]).then_inc(S.fac, 16)
-    g.scalar.dma_start(T.vtb[:, :], T.vt[:, :]).then_inc(S.fac, 16)
-    g.sync.dma_start(T.xb[:, 0:CW], T.x[:, 0:CW]).then_inc(S.xl, 16)
-    g.scalar.dma_start(T.xb[:, CW:TK], T.x[:, CW:TK]).then_inc(S.xl, 16)
+    g.sync.dma_start(T.fac[0, 0:HR, :], T.ut[:, :]).then_inc(S.stg, 16)
+    g.scalar.dma_start(T.fac[0, HR:P, :], T.vt[:, :]).then_inc(S.stg, 16)
+    g.sync.dma_start(T.fu[0:R, :], T.ut[:, :]).then_inc(S.ld, 16)
+    g.scalar.dma_start(T.fv[0:R, :], T.vt[:, :]).then_inc(S.ld, 16)
+    g.sync.dma_start(T.xb[0:HR, :], T.x[0:HR, :]).then_inc(S.xl, 16)
+    g.scalar.dma_start(T.xb[HR:P, :], T.x[HR:P, :]).then_inc(S.xl, 16)
 
-    g.tensor.wait_ge(S.fac, 32)
-    g.tensor.matmul(T.pw[:, 0:P], T.utb[:, :], T.vtb[:, :], True, True).then_inc(S.mmw, 1)
+    g.tensor.wait_ge(S.ld, 32)
+    g.tensor.matmul(T.pw[:, 0:P], T.fu[0:R, :], T.fv[0:R, :], True, True).then_inc(S.mmw, 1)
     g.vector.wait_ge(S.mmw, 1)
     g.vector.tensor_copy(T.wown[:, :], T.pw[:, 0:P]).then_inc(S.cw, 1)
 
     sent = 0
+    g.wait_ge(S.stg, 32)
+    tds = _thin_dsts(topo, group, core)
+    if tds:
+        g.remote_dma_fused(
+            [RemoteDMATransfer(dst_ids=[did(d) for d in tds], dma_engine_mask=_bits(use), remote_sem=S.thin,
+                               srcs=[T.fac[0]], dsts=[T.fac[1 + idx(d, core)] for d in tds], alu_op=0)],
+            local_sem=S.sent)
+        sent += len(use)
     g.wait_ge(S.cw, 1)
-    for call in _near_calls(topo, group, core):
+    ww = _w_writes(topo, group, core)
+    if ww:
         g.remote_dma_fused(
             [RemoteDMATransfer(dst_ids=[did(d)], dma_engine_mask=_bits(es), remote_sem=S.on,
-                               src=T.wown[:, :], dst=slot(d, core)) for d, es in call],
+                               src=T.wown[:, :], dst=wslot(d, core)) for d, es in ww],
             local_sem=S.sent)
-        sent += sum(len(es) for d, es in call)
-    g.wait_ge(S.on, on_total)
-    if core in ports:
+        sent += sum(len(es) for _, es in ww)
+    if is_port:
+        g.wait_ge(S.on, on_total)
         share = _far_share(topo, group, core)
-        es = _engs(topo, core, share[0])
         g.remote_dma_fused(
-            [RemoteDMATransfer(dst_ids=[did(d) for d in share], dma_engine_mask=_bits(es), remote_sem=S.off,
-                               srcs=[T.wown[:, :]] + [slot(core, s) for s in others],
+            [RemoteDMATransfer(dst_ids=[did(d) for d in share], dma_engine_mask=_bits(use), remote_sem=S.off,
+                               srcs=[T.wown[:, :]] + [wslot(core, s) for s in others],
                                dsts=[T.woff[:, :] for d in share], alu_op=1)],
             local_sem=S.sent)
-        sent += len(es)
+        sent += len(use)
 
-    py = [T.py0, T.py1]
-    my = [S.my0, S.my1]
-    cy = [S.cy0, S.cy1]
-    xs = [T.xb[:, b * CW:(b + 1) * CW] for b in range(NCH)]
-    g.tensor.wait_ge(S.cw, 1)
-    g.tensor.wait_ge(S.xl, 32)
-    for b in range(NCH):
-        g.tensor.matmul(py[b][:, 0:CW], T.wown[:, :], xs[b], True, False)
-    g.tensor.wait_ge(S.on, on_total)
-    for s in others:
-        for b in range(NCH):
-            g.tensor.matmul(py[b][:, 0:CW], slot(core, s), xs[b], False, False)
+    py = [T["py%d" % b] for b in range(NB)]
+    xs = [T.xb[:, b * CW:(b + 1) * CW] for b in range(NB)]
+    if is_port:
+        g.tensor.wait_ge(S.cw, 1)
+        g.tensor.wait_ge(S.xl, 32)
+        for b in range(NB):
+            g.tensor.matmul(py[b][:, 0:CW], T.wown[:, :], xs[b], True, False)
+        g.tensor.wait_ge(S.on, on_total)
+        for s in others:
+            for b in range(NB):
+                g.tensor.matmul(py[b][:, 0:CW], wslot(core, s), xs[b], False, False)
+    else:
+        k = (1 + len(others)) * R
+        for q, buf, lo, hi in ((g.sync, T.fu, 0, HR), (g.scalar, T.fv, HR, P)):
+            q.wait_ge(S.thin, thin_total)
+            q.dma_start(buf[R:k, :], T.fac[1:1 + len(others), lo:hi, :]).then_inc(S.l2, 16)
+        g.tensor.wait_ge(S.l2, 32)
+        g.tensor.matmul(T.pn[:, 0:P], T.fu[0:k, :], T.fv[0:k, :], True, True).then_inc(S.mmn, 1)
+        g.vector.wait_ge(S.mmn, 1)
+        g.vector.tensor_copy(T.wnear[:, :], T.pn[:, 0:P]).then_inc(S.cn, 1)
+        g.tensor.wait_ge(S.cn, 1)
+        g.tensor.wait_ge(S.xl, 32)
+        for b in range(NB):
+            g.tensor.matmul(py[b][:, 0:CW], T.wnear[:, :], xs[b], True, False)
+
     g.tensor.wait_ge(S.off, off_total)
-    for b in range(NCH):
-        g.tensor.matmul(py[b][:, 0:CW], T.woff[:, :], xs[b], False, True).then_inc(my[b], 1)
+    for b in range(NB):
+        g.tensor.matmul(py[b][:, 0:CW], T.woff[:, :], xs[b], False, True).then_inc(S["my%d" % b], 1)
 
-    queues = [g.sync, g.scalar]
-    for b in range(NCH):
-        g.vector.wait_ge(my[b], 1)
-        g.vector.tensor_copy(T.yb[:, b * CW:(b + 1) * CW], py[b][:, 0:CW]).then_inc(cy[b], 1)
-        queues[b].wait_ge(cy[b], 1)
-        queues[b].dma_start(T.y[:, b * CW:(b + 1) * CW], T.yb[:, b * CW:(b + 1) * CW]).then_inc(S.st, 16)
+    for b in range(NB):
+        dst, src = T.yb[:, b * CW:(b + 1) * CW], py[b][:, 0:CW]
+        if b % 2 == 0:
+            g.vector.wait_ge(S["my%d" % b], 1)
+            g.vector.tensor_copy(dst, src).then_inc(S["cy%d" % b], 1)
+        else:
+            g.scalar.wait_ge(S["my%d" % b], 1)
+            g.scalar.activation(dst, src, ActivationFunctionType.Copy).then_inc(S["cy%d" % b], 1)
+
+    half = NB // 2
+    for h, q in enumerate((g.sync, g.scalar)):
+        for b in range(h * half, (h + 1) * half):
+            q.wait_ge(S["cy%d" % b], 1)
+        q.dma_start(T.y[:, h * half * CW:(h + 1) * half * CW],
+                    T.yb[:, h * half * CW:(h + 1) * half * CW]).then_inc(S.st, 16)
 
     g.wait_ge(S.sent, sent)
+    if thin_total:
+        g.wait_ge(S.thin, thin_total)
     g.wait_ge(S.off, off_total)
-    g.wait_ge(S.st, 16 * NCH)
+    g.wait_ge(S.st, 32)

import comms_topo
from concourse.bass import DstId, RemoteDMATransfer
from concourse.mybir import ActivationFunctionType

CORES = [100, 101, 102, 103, 108, 109, 110, 111]
P, R, TK = 128, 16, 512
PW = 2 * R
HR = P // 2
NB = 4
CW = TK // NB
SLOTS = max(sum(1 for d in CORES if comms_topo.chip(d) == comms_topo.chip(c)) for c in CORES) - 1

SCRATCH = {
    "fac": ("dram", [SLOTS + 1, P, PW], "bfloat16"),
    "fu": ("sbuf", [(SLOTS + 1) * R, P], "bfloat16"),
    "fv": ("sbuf", [(SLOTS + 1) * R, P], "bfloat16"),
    "xb": ("sbuf", [P, TK], "bfloat16"),
    "wown": ("sbuf", [P, P], "bfloat16"),
    "wnear": ("sbuf", [P, P], "bfloat16"),
    "wpeer": ("sbuf", [P, SLOTS * P], "bfloat16"),
    "woff": ("sbuf", [P, P], "bfloat16"),
    "yb": ("sbuf", [P, TK], "bfloat16"),
    "pw": ("psum", [P, 512], "float32"),
    "pn": ("psum", [P, 512], "float32"),
    "py0": ("psum", [P, 512], "float32"),
    "py1": ("psum", [P, 512], "float32"),
    "py2": ("psum", [P, 512], "float32"),
    "py3": ("psum", [P, 512], "float32"),
}
SEMAPHORES = ["stg", "ld", "xl", "mmw", "cw", "thin", "l2", "mmn", "cn", "on", "off", "sent",
              "my0", "my1", "my2", "my3", "cy0", "cy1", "cy2", "cy3", "st"]


def _engs(topo, src, dst):
    m = topo.mask(src, dst)
    return [e for e in range(m.bit_length()) if (m >> e) & 1]


def _bits(es):
    return sum(1 << e for e in es)


def _split(es, dsts):
    if not dsts:
        return []
    n = 1
    while 2 * n * len(dsts) <= len(es):
        n *= 2
    return [(d, es[i * n:(i + 1) * n]) for i, d in enumerate(dsts)]


def _sides(topo, group, c):
    near = [d for d in group if topo.chip(d) == topo.chip(c)]
    far = [d for d in group if topo.chip(d) != topo.chip(c)]
    ports = [d for d in near if all(topo.may_write(d, f) for f in far)]
    return near, far, ports


def _use(topo, group, s):
    near, far, ports = _sides(topo, group, s)
    return _engs(topo, s, far[0]) if s in ports else _engs(topo, s, [c for c in near if c != s][0])


def _thin_dsts(topo, group, s):
    near, _, ports = _sides(topo, group, s)
    return [c for c in near if c != s and c not in ports]


def _w_writes(topo, group, s):
    _, _, ports = _sides(topo, group, s)
    return _split(_use(topo, group, s), [c for c in ports if c != s])


def _far_share(topo, group, s):
    _, far, ports = _sides(topo, group, s)
    return far[ports.index(s)::len(ports)]


def rank_program(g, core, T, topo):
    if T.rank_of(core) is None:
        return
    S = T.sem
    group = list(T.cores)
    near, far, ports = _sides(topo, group, core)
    others = [c for c in near if c != core]
    is_port = core in ports
    use = _use(topo, group, core)

    def idx(dst, src):
        return [c for c in near if c != dst].index(src)

    def wslot(dst, src):
        k = idx(dst, src)
        return T.wpeer[:, k * P:(k + 1) * P]

    def did(c):
        rid, pid, _ = topo.addr(c)
        return DstId(rid=rid, pnc=pid)

    thin_total = sum(len(_use(topo, group, s)) for s in others if core in _thin_dsts(topo, group, s))
    on_total = sum(len(es) for s in others for d, es in _w_writes(topo, group, s) if d == core)
    feeder = [s for s in _sides(topo, group, far[0])[2] if core in _far_share(topo, group, s)][0]
    off_total = len(_use(topo, group, feeder))

    g.sync.dma_start(T.fac[0, 0:HR, :], T.ut[:, :]).then_inc(S.stg, 16)
    g.scalar.dma_start(T.fac[0, HR:P, :], T.vt[:, :]).then_inc(S.stg, 16)
    g.sync.dma_start(T.fu[0:R, :], T.ut[:, :]).then_inc(S.ld, 16)
    g.scalar.dma_start(T.fv[0:R, :], T.vt[:, :]).then_inc(S.ld, 16)
    g.sync.dma_start(T.xb[0:HR, :], T.x[0:HR, :]).then_inc(S.xl, 16)
    g.scalar.dma_start(T.xb[HR:P, :], T.x[HR:P, :]).then_inc(S.xl, 16)

    g.tensor.wait_ge(S.ld, 32)
    g.tensor.matmul(T.pw[:, 0:P], T.fu[0:R, :], T.fv[0:R, :], True, True).then_inc(S.mmw, 1)
    g.vector.wait_ge(S.mmw, 1)
    g.vector.tensor_copy(T.wown[:, :], T.pw[:, 0:P]).then_inc(S.cw, 1)

    sent = 0
    g.wait_ge(S.stg, 32)
    tds = _thin_dsts(topo, group, core)
    if tds:
        g.remote_dma_fused(
            [RemoteDMATransfer(dst_ids=[did(d) for d in tds], dma_engine_mask=_bits(use), remote_sem=S.thin,
                               srcs=[T.fac[0]], dsts=[T.fac[1 + idx(d, core)] for d in tds], alu_op=0)],
            local_sem=S.sent)
        sent += len(use)
    g.wait_ge(S.cw, 1)
    ww = _w_writes(topo, group, core)
    if ww:
        g.remote_dma_fused(
            [RemoteDMATransfer(dst_ids=[did(d)], dma_engine_mask=_bits(es), remote_sem=S.on,
                               src=T.wown[:, :], dst=wslot(d, core)) for d, es in ww],
            local_sem=S.sent)
        sent += sum(len(es) for _, es in ww)
    if is_port:
        g.wait_ge(S.on, on_total)
        share = _far_share(topo, group, core)
        g.remote_dma_fused(
            [RemoteDMATransfer(dst_ids=[did(d) for d in share], dma_engine_mask=_bits(use), remote_sem=S.off,
                               srcs=[T.wown[:, :]] + [wslot(core, s) for s in others],
                               dsts=[T.woff[:, :] for d in share], alu_op=1)],
            local_sem=S.sent)
        sent += len(use)

    py = [T["py%d" % b] for b in range(NB)]
    xs = [T.xb[:, b * CW:(b + 1) * CW] for b in range(NB)]
    if is_port:
        g.tensor.wait_ge(S.cw, 1)
        g.tensor.wait_ge(S.xl, 32)
        for b in range(NB):
            g.tensor.matmul(py[b][:, 0:CW], T.wown[:, :], xs[b], True, False)
        g.tensor.wait_ge(S.on, on_total)
        for s in others:
            for b in range(NB):
                g.tensor.matmul(py[b][:, 0:CW], wslot(core, s), xs[b], False, False)
    else:
        k = (1 + len(others)) * R
        for q, buf, lo, hi in ((g.sync, T.fu, 0, HR), (g.scalar, T.fv, HR, P)):
            q.wait_ge(S.thin, thin_total)
            q.dma_start(buf[R:k, :], T.fac[1:1 + len(others), lo:hi, :]).then_inc(S.l2, 16)
        g.tensor.wait_ge(S.l2, 32)
        g.tensor.matmul(T.pn[:, 0:P], T.fu[0:k, :], T.fv[0:k, :], True, True).then_inc(S.mmn, 1)
        g.vector.wait_ge(S.mmn, 1)
        g.vector.tensor_copy(T.wnear[:, :], T.pn[:, 0:P]).then_inc(S.cn, 1)
        g.tensor.wait_ge(S.cn, 1)
        g.tensor.wait_ge(S.xl, 32)
        for b in range(NB):
            g.tensor.matmul(py[b][:, 0:CW], T.wnear[:, :], xs[b], True, False)

    g.tensor.wait_ge(S.off, off_total)
    for b in range(NB):
        g.tensor.matmul(py[b][:, 0:CW], T.woff[:, :], xs[b], False, True).then_inc(S["my%d" % b], 1)

    for b in range(NB):
        dst, src = T.yb[:, b * CW:(b + 1) * CW], py[b][:, 0:CW]
        if b % 2 == 0:
            g.vector.wait_ge(S["my%d" % b], 1)
            g.vector.tensor_copy(dst, src).then_inc(S["cy%d" % b], 1)
        else:
            g.scalar.wait_ge(S["my%d" % b], 1)
            g.scalar.activation(dst, src, ActivationFunctionType.Copy).then_inc(S["cy%d" % b], 1)

    half = NB // 2
    for h, q in enumerate((g.sync, g.scalar)):
        for b in range(h * half, (h + 1) * half):
            q.wait_ge(S["cy%d" % b], 1)
        q.dma_start(T.y[:, h * half * CW:(h + 1) * half * CW],
                    T.yb[:, h * half * CW:(h + 1) * half * CW]).then_inc(S.st, 16)

    g.wait_ge(S.sent, sent)
    if thin_total:
        g.wait_ge(S.thin, thin_total)
    g.wait_ge(S.off, off_total)
    g.wait_ge(S.st, 32)
